import numpy as np
import ml_dtypes


def mxq(x, axis, fmt="e4m3"):
    dtype, down = {"e4m3": (ml_dtypes.float8_e4m3fn, 7), "e5m2": (ml_dtypes.float8_e5m2, 14)}[fmt]
    v = np.moveaxis(np.asarray(x, np.float32).astype(ml_dtypes.bfloat16).astype(np.float64), axis, -1)
    blocks = v.reshape(v.shape[:-1] + (-1, 32))
    amax = np.abs(blocks).max(-1, keepdims=True)
    byte = np.maximum(np.where(amax > 0, np.frexp(amax)[1] - 1 + 127, 0) - down, 1)
    scale = np.exp2(byte - 127.0)
    codes = (blocks / scale).astype(np.float32).astype(dtype).astype(np.float64)
    return np.moveaxis((codes * scale).reshape(v.shape), -1, axis)


WIDE = False


def mx_kscale(k):
    if not WIDE:
        return np.ones(k)
    levels = np.array([10, -10, 5, -5, 0])
    if k % 512:
        return np.exp2(np.random.permutation(np.resize(levels, k // 32))).repeat(32)
    a = np.empty((k // 512, 16))
    for p in range(k // 512):
        a[p, :8] = np.random.permutation(np.resize(levels, 8))
        for g in range(8):
            far = levels[np.abs(levels - a[p, g]) >= 10]
            a[p, g + 8] = far[np.random.randint(len(far))]
    return np.exp2(a.ravel()).repeat(32)


def f64(x):
    return np.asarray(x).astype(np.float64)


def striped(idx):
    return np.tile(idx.reshape(-1, 16).T, (8, 1)).astype(np.uint16)


def unstriped(offs):
    return offs[:16].T.reshape(-1).astype(np.int64)


def striped8(idx):
    return np.concatenate([x.reshape(-1, 16).T for x in idx]).astype(np.uint16)


def runs(offs, k):
    lists = np.stack([offs[16 * r : 16 * r + 16].T.reshape(-1) for r in range(8)]).astype(np.int64)
    return lists[np.arange(k) % 512 // 64]


def pack_weight(w):
    k, n = w.shape
    w = f64(np.asarray(w, np.float32).astype(ml_dtypes.bfloat16)).reshape(k // 32, 32, n)
    amax = np.abs(w).max(1)
    byte = np.clip(np.where(amax > 0, np.frexp(amax)[1] - 1 + 127 - 7, 1), 1, 254)
    scaled = (w * np.exp2(127.0 - byte)[:, None, :]).reshape(k, n).astype(np.float32)
    words = np.ascontiguousarray(scaled.reshape(k // 512, 128, 4, n).transpose(0, 1, 3, 2)).astype(ml_dtypes.float8_e4m3fn).view(np.uint8)
    return words, np.ascontiguousarray(byte.astype(np.uint8).reshape(k // 512, 16, n))


def unpack_weight(words, scales):
    g, p, n, _ = words.shape
    vals = np.ascontiguousarray(words).view(ml_dtypes.float8_e4m3fn).astype(np.float64) * np.repeat(np.exp2(scales.astype(np.float64) - 127.0), 8, axis=1)[..., None]
    return vals.transpose(0, 1, 3, 2).reshape(g * 512, n)


def sigmoid(v):
    return 1.0 / (1.0 + np.exp(-np.maximum(v, -700.0)))


K, T, S, N, G, H = 512, 2048, 512, 512, 2048, 512


def setup_inputs():
    n = np.random.standard_normal
    s = mx_kscale(K)[:, None]
    u = mx_kscale(S)
    packed_xT = pack_weight(n((K, T)) * s)
    packed_dT = pack_weight(n((K, G)) / s)
    return {
        "x_words": packed_xT[0],
        "x_scales": packed_xT[1],
        "d_words": packed_dT[0],
        "d_scales": packed_dT[1],
        "gn": (np.random.uniform(0.5, 1.5, (H, 1)) * u[:, None]).astype(np.float32),
        "w1": (n((H, N)) / np.sqrt(H) / u[:, None]).astype(np.float32),
        "offs": striped(np.random.permutation(T)[:S]),
        "kidx": striped8(np.random.randint(0, G, (8, H))),
        "n1": striped8(np.stack([np.random.permutation(S) for _ in range(8)])),
        "n2": striped8(np.stack([np.random.permutation(S) for _ in range(8)])),
    }


def reference(x_words, x_scales, d_words, d_scales, gn, w1, offs, kidx, n1, n2):
    d_kidx = unpack_weight(d_words, d_scales)[np.arange(K)[:, None], runs(kidx, K)]
    xq = unpack_weight(x_words, x_scales)[:, unstriped(offs)]
    s = 0.0625 * (d_kidx.T @ xq)
    st = s - (s[np.arange(H)[:, None], runs(n1, H)])
    z = f64(gn) * (st - (0.5 * (st[np.arange(H)[:, None], runs(n1, H)])))
    h = mxq(f64(w1), 0, "e4m3").T @ mxq(z, 0, "e4m3")
    st2 = h * (sigmoid(h[np.arange(N)[:, None], runs(n2, N)]))
    return np.maximum(st2, st2[np.arange(N)[:, None], runs(n2, N)])

@@ -1,0 +1,196 @@
+from contextlib import ExitStack
+
+import concourse.mybir as mybir
+
+K, T, S, N, G, H = 512, 2048, 512, 512, 2048, 512
+FLOPS = 2 * K * H * S + 2 * H * N * S
+
+F32 = mybir.dt.float32
+BF16 = mybir.dt.bfloat16
+I32 = mybir.dt.int32
+U32 = mybir.dt.uint32
+U16 = mybir.dt.uint16
+U8 = mybir.dt.uint8
+FP8X4 = mybir.dt.float8_e4m3fn_x4
+ALU = mybir.AluOpType
+ACT = mybir.ActivationFunctionType
+
+P = 128
+PACK = 4
+PIECES = ((0, 256), (256, 128), (384, 128))
+
+
+def tile_picked_keytwicetwicp_none_p_kernel(
+    tc, x_words, x_scales, d_words, d_scales, gn, w1, offs, kidx, n1, n2, out
+):
+    nc = tc.nc
+    with ExitStack() as ctx:
+        lists = ctx.enter_context(tc.tile_pool(name="lists", bufs=1))
+        sb = ctx.enter_context(tc.tile_pool(name="sb", bufs=1))
+        psum = ctx.enter_context(tc.psum_pool(name="psum", bufs=1))
+
+        def tile(name, shape, dtype):
+            return sb.tile(shape, dtype, name=name, align_bytes=64)
+
+        def entries(list_tile, first, count):
+            return list_tile[:, first // 16 : (first + count) // 16]
+
+        kidx_sb = lists.tile([P, H // 16], U16, name="kidx_sb")
+        offs_sb = lists.tile([P, S // 16], U16, name="offs_sb")
+        n1_sb = lists.tile([P, S // 16], U16, name="n1_sb")
+        n2_sb = lists.tile([P, S // 16], U16, name="n2_sb")
+
+        d_scale_table = tile("d_scale_table", [P, G], U8)
+        x_scale_table = tile("x_scale_table", [P, T], U8)
+        d_table = tile("d_table", [P, G], U32)
+        x_table = tile("x_table", [P, T], U32)
+        nc.vector.memset(d_scale_table[:].bitcast(I32), 0)
+        nc.vector.memset(x_scale_table[:].bitcast(I32), 0)
+
+        gain = tile("gain", [P, PACK], F32)
+        w_raw = tile("w_raw", [P, PACK, N], F32)
+        nc.sync.dma_start(kidx_sb[:], kidx)
+        nc.sync.dma_start(offs_sb[:], offs)
+        nc.sync.dma_start(n1_sb[:], n1)
+        nc.sync.dma_start(n2_sb[:], n2)
+        nc.sync.dma_start(gain[:], gn.rearrange("(p t) o -> p (t o)", t=PACK))
+        d_rows = d_scales[0].bitcast(I32).rearrange("(r a) n -> a r n", a=2)
+        for a in range(2):
+            nc.sync.dma_start(d_scale_table[a:P:16, :].bitcast(I32), d_rows[a])
+        nc.sync.dma_start(d_table[:].bitcast(I32), d_words[0].rearrange("p n t -> p (n t)").bitcast(I32))
+        x_rows = x_scales[0].bitcast(I32).rearrange("(q a) n -> a q n", a=4)
+        for a in range(4):
+            nc.sync.dma_start(x_scale_table[a:P:32, :].bitcast(I32), x_rows[a])
+        nc.sync.dma_start(x_table[:].bitcast(I32), x_words[0].rearrange("p n t -> p (n t)").bitcast(I32))
+        nc.sync.dma_start(w_raw[:], w1.rearrange("(p j) m -> p j m", j=PACK))
+
+        d_scale_picked = tile("d_scale_picked", [P, H], U8)
+        nc.vector.tensor_copy(d_scale_picked[:], d_scale_table[:].indirect(kidx_sb[:]))
+        d_scale_dealt = tile("d_scale_dealt", [P, H], U8)
+        nc.vector.tensor_copy(
+            d_scale_dealt[:].rearrange("p (t m) -> p m t", t=PACK),
+            d_scale_picked[:].rearrange("p (m t) -> p m t", t=PACK),
+        )
+        key_scales = tile("key_scales", [P, H], U8)
+        nc.vector.tensor_copy(key_scales[:].bitcast(I32), d_scale_dealt[:].bitcast(I32))
+        nc.scalar.dma_start(key_scales[2:P:32, :].bitcast(I32), d_scale_dealt[16:P:32, :].bitcast(I32))
+        nc.scalar.dma_start(key_scales[3:P:32, :].bitcast(I32), d_scale_dealt[17:P:32, :].bitcast(I32))
+
+        d_picked = tile("d_picked", [P, H], U32)
+        nc.vector.tensor_copy(d_picked[:], d_table[:].indirect(kidx_sb[:]))
+        key_words = tile("key_words", [P, H], U32)
+        nc.vector.tensor_copy(
+            key_words[:].rearrange("p (t m) -> p m t", t=PACK),
+            d_picked[:].rearrange("p (m t) -> p m t", t=PACK),
+        )
+        query_scales = tile("query_scales", [P, S], U8)
+        nc.vector.tensor_copy(query_scales[:], x_scale_table[:].indirect(offs_sb[:]))
+        half = S // 2
+        query_words = [tile("query_words%d" % u, [P, half], U32) for u in range(2)]
+        for u in range(2):
+            nc.vector.tensor_copy(query_words[u][:], x_table[:].indirect(entries(offs_sb, u * half, half)))
+
+        row_scale = tile("row_scale", [P, PACK], F32)
+        nc.scalar.activation(row_scale[:], gain[:], ACT.Copy, scale=1.0 / 32.0)
+
+        banks = [psum.tile([P, 512], F32, name="bank%d" % b) for b in range(8)]
+        s_window = [tile("s_window0", [P, S], F32)] + [tile("s_window%d" % t, [P, 2 * S], F32) for t in range(1, PACK)]
+        s_plain = [s_window[t + 1][:, S:] for t in range(PACK - 1)] + [tile("s_plain3", [P, S], F32)[:]]
+        for u in range(2):
+            for t in range(PACK):
+                nc.tensor.matmul_mx(
+                    out=banks[2 * t + u][:, :half],
+                    lhsT=key_words[:, t * P : (t + 1) * P].bitcast(FP8X4),
+                    lhsT_scale=key_scales[:, t * P : (t + 1) * P],
+                    rhs=query_words[u][:].bitcast(FP8X4),
+                    rhs_scale=query_scales[:, u * half : (u + 1) * half],
+                    start=True,
+                    stop=True,
+                )
+
+        a_window = [tile("a_window%d" % t, [P, S], F32) for t in range(PACK)]
+        h_window = [tile("h_window%d" % t, [P, 2 * S], F32) for t in range(PACK)]
+        w_grouped = tile("w_grouped", [P, N * PACK], BF16)
+        w_words = tile("w_words", [P, N], U32)
+        w_scales = tile("w_scales", [P, N], U8)
+        for t in range(PACK):
+            for u in range(2):
+                cols = slice(u * half, (u + 1) * half)
+                src = banks[2 * t + u][:, :half]
+                nc.scalar.activation(s_window[t][:, cols], src, ACT.Copy, scale=row_scale[:, t : t + 1])
+                nc.scalar.activation(s_plain[t][:, cols], src, ACT.Copy, scale=row_scale[:, t : t + 1])
+            if t == 0:
+                for u in range(2):
+                    cols = slice(u * half, (u + 1) * half)
+                    nc.vector.tensor_tensor(
+                        a_window[t][:, cols],
+                        s_window[t][:].indirect(entries(n1_sb, u * half, half)),
+                        s_plain[t][:, cols],
+                        ALU.subtract,
+                    )
+            else:
+                nc.vector.tensor_tensor(a_window[t][:], s_window[t][:].indirect(n1_sb[:]), s_plain[t], ALU.subtract)
+            if t < 2:
+                m0, m1 = t * (P // 2), (t + 1) * (P // 2)
+                nc.vector.tensor_copy(
+                    w_grouped[:].rearrange("p (t m j) -> p m t j", t=PACK, j=PACK)[:, m0:m1],
+                    w_raw[:].rearrange("p j (m t) -> p m t j", t=PACK)[:, m0:m1],
+                )
+            if t == 2:
+                nc.vector.quantize_mx(out=w_words[:].bitcast(FP8X4), scales=w_scales[:], in_=w_grouped[:])
+        for t in range(PACK):
+            nc.scalar.activation(h_window[t][:, S:], a_window[t][:], ACT.Copy, scale=2.0)
+
+        h_banks = [psum.tile([P, 512], F32, name="bank%d" % b) for b in range(7)]
+        h_place = [
+            [h_banks[t // 2][:, (t % 2) * 256 : (t % 2 + 1) * 256] for t in range(PACK)],
+            [h_banks[2][:, t * 128 : (t + 1) * 128] for t in range(PACK)],
+            [h_banks[3 + t][:, :128] for t in range(PACK)],
+        ]
+        last = len(PIECES) - 1
+        for c, (first, count) in enumerate(PIECES):
+            cols = slice(first, first + count)
+            z_planes = tile("z_planes%d" % c, [P, PACK, count], F32)
+            for t in range(PACK):
+                nc.vector.tensor_tensor(
+                    z_planes[:, t, :],
+                    a_window[t][:].indirect(entries(n1_sb, first, count)),
+                    h_window[t][:, S + first : S + first + count],
+                    ALU.subtract,
+                )
+            z_grouped = tile("z_grouped%d" % c, [P, count * PACK], BF16)
+            dst = z_grouped[:].rearrange("p (c i t) -> p c t i", i=4, t=PACK)
+            src = z_planes[:].rearrange("p t (c i) -> p c t i", i=4)
+            if c == last:
+                nc.vector.tensor_copy(dst, src)
+            else:
+                nc.scalar.copy(dst, src)
+            z_words = tile("z_words%d" % c, [P, count], U32)
+            z_scales = tile("z_scales%d" % c, [P, count], U8)
+            nc.vector.quantize_mx(out=z_words[:].bitcast(FP8X4), scales=z_scales[:], in_=z_grouped[:])
+            for t in range(PACK):
+                nc.tensor.matmul_mx(
+                    out=h_place[c][t],
+                    lhsT=w_words[:, t * P : (t + 1) * P].bitcast(FP8X4),
+                    lhsT_scale=w_scales[:, t * P : (t + 1) * P],
+                    rhs=z_words[:].bitcast(FP8X4),
+                    rhs_scale=z_scales[:],
+                    start=True,
+                    stop=True,
+                )
+            for t in range(PACK):
+                if c == last and t > 0:
+                    nc.vector.tensor_copy(h_window[t][:, cols], h_place[c][t])
+                else:
+                    nc.scalar.copy(h_window[t][:, cols], h_place[c][t])
+
+        out_rows = out.rearrange("(p t) j -> t p j", t=PACK)
+        for t in range(PACK):
+            st2_window = tile("st2_window%d" % t, [P, 2 * S], F32)
+            nc.scalar.activation(st2_window[:, S:], h_window[t][:].indirect(n2_sb[:]), ACT.Sigmoid)
+            nc.vector.tensor_tensor(st2_window[:, :S], h_window[t][:, :S], st2_window[:, S:], ALU.mult)
+            fetched = tile("fetched%d" % t, [P, S], F32)
+            nc.vector.tensor_copy(fetched[:], st2_window[:].indirect(n2_sb[:]))
+            result = tile("result%d" % t, [P, S], F32)
+            nc.vector.tensor_tensor(result[:], st2_window[:, :S], fetched[:], ALU.max)
+            nc.sync.dma_start(out_rows[t], result[:])

@@ -17,6 +17,7 @@ ACT = mybir.ActivationFunctionType
 
 P = 128
 PACK = 4
+W_SPLIT = 64
 PIECES = ((0, 256), (256, 128), (384, 128))
 
 
@@ -41,28 +42,30 @@ def tile_picked_keytwicetwicp_none_p_kernel(
         n2_sb = lists.tile([P, S // 16], U16, name="n2_sb")
 
         d_scale_table = tile("d_scale_table", [P, G], U8)
-        x_scale_table = tile("x_scale_table", [P, T], U8)
-        d_table = tile("d_table", [P, G], U32)
+        x_scale_table = sb.tile([P, T], U8, name="x_scale_table", tag="x_scales_then_words", align_bytes=64)
+        key_scales = tile("key_scales", [P, H], U8)
+        d_table = sb.tile([P, G], U32, name="d_table", tag="d_then_w", align_bytes=64)
         x_table = tile("x_table", [P, T], U32)
+        gain = tile("gain", [P, PACK], F32)
+        warm = tile("warm", [P, 8], F32)
         nc.vector.memset(d_scale_table[:].bitcast(I32), 0)
         nc.vector.memset(x_scale_table[:].bitcast(I32), 0)
+        nc.gpsimd.memset(warm[:, 0:1], 0.0)
+        nc.scalar.activation(warm[:, 4:5], warm[:, 0:1], ACT.Sigmoid)
 
-        gain = tile("gain", [P, PACK], F32)
-        w_raw = tile("w_raw", [P, PACK, N], F32)
         nc.sync.dma_start(kidx_sb[:], kidx)
-        nc.sync.dma_start(offs_sb[:], offs)
-        nc.sync.dma_start(n1_sb[:], n1)
-        nc.sync.dma_start(n2_sb[:], n2)
-        nc.sync.dma_start(gain[:], gn.rearrange("(p t) o -> p (t o)", t=PACK))
         d_rows = d_scales[0].bitcast(I32).rearrange("(r a) n -> a r n", a=2)
         for a in range(2):
             nc.sync.dma_start(d_scale_table[a:P:16, :].bitcast(I32), d_rows[a])
+        nc.sync.dma_start(offs_sb[:], offs)
         nc.sync.dma_start(d_table[:].bitcast(I32), d_words[0].rearrange("p n t -> p (n t)").bitcast(I32))
         x_rows = x_scales[0].bitcast(I32).rearrange("(q a) n -> a q n", a=4)
         for a in range(4):
-            nc.sync.dma_start(x_scale_table[a:P:32, :].bitcast(I32), x_rows[a])
+            nc.scalar.dma_start(x_scale_table[a:P:32, :].bitcast(I32), x_rows[a])
         nc.sync.dma_start(x_table[:].bitcast(I32), x_words[0].rearrange("p n t -> p (n t)").bitcast(I32))
-        nc.sync.dma_start(w_raw[:], w1.rearrange("(p j) m -> p j m", j=PACK))
+        nc.sync.dma_start(gain[:], gn.rearrange("(p t) o -> p (t o)", t=PACK))
+        nc.sync.dma_start(n1_sb[:], n1)
+        nc.sync.dma_start(n2_sb[:], n2)
 
         d_scale_picked = tile("d_scale_picked", [P, H], U8)
         nc.vector.tensor_copy(d_scale_picked[:], d_scale_table[:].indirect(kidx_sb[:]))
@@ -71,126 +74,153 @@ def tile_picked_keytwicetwicp_none_p_kernel(
             d_scale_dealt[:].rearrange("p (t m) -> p m t", t=PACK),
             d_scale_picked[:].rearrange("p (m t) -> p m t", t=PACK),
         )
-        key_scales = tile("key_scales", [P, H], U8)
         nc.vector.tensor_copy(key_scales[:].bitcast(I32), d_scale_dealt[:].bitcast(I32))
-        nc.scalar.dma_start(key_scales[2:P:32, :].bitcast(I32), d_scale_dealt[16:P:32, :].bitcast(I32))
-        nc.scalar.dma_start(key_scales[3:P:32, :].bitcast(I32), d_scale_dealt[17:P:32, :].bitcast(I32))
+        for a in range(2):
+            nc.scalar.dma_start(key_scales[2 + a : P : 32, :].bitcast(I32), d_scale_dealt[16 + a : P : 32, :].bitcast(I32))
 
         d_picked = tile("d_picked", [P, H], U32)
         nc.vector.tensor_copy(d_picked[:], d_table[:].indirect(kidx_sb[:]))
+        w_raw = sb.tile([P, PACK, N], F32, name="w_raw", tag="d_then_w", align_bytes=64)
+        nc.sync.dma_start(w_raw[:], w1.rearrange("(p j) m -> p j m", j=PACK))
+        query_scales = tile("query_scales", [P, S], U8)
+        nc.vector.tensor_copy(query_scales[:], x_scale_table[:].indirect(offs_sb[:]))
         key_words = tile("key_words", [P, H], U32)
         nc.vector.tensor_copy(
             key_words[:].rearrange("p (t m) -> p m t", t=PACK),
             d_picked[:].rearrange("p (m t) -> p m t", t=PACK),
         )
-        query_scales = tile("query_scales", [P, S], U8)
-        nc.vector.tensor_copy(query_scales[:], x_scale_table[:].indirect(offs_sb[:]))
         half = S // 2
-        query_words = [tile("query_words%d" % u, [P, half], U32) for u in range(2)]
+        halves = [slice(0, half), slice(half, S)]
+        query_words = [
+            sb.tile([P, half], U32, name="query_words0", tag="x_scales_then_words", align_bytes=64),
+            tile("query_words1", [P, half], U32),
+        ]
         for u in range(2):
             nc.vector.tensor_copy(query_words[u][:], x_table[:].indirect(entries(offs_sb, u * half, half)))
 
         row_scale = tile("row_scale", [P, PACK], F32)
         nc.scalar.activation(row_scale[:], gain[:], ACT.Copy, scale=1.0 / 32.0)
 
-        banks = [psum.tile([P, 512], F32, name="bank%d" % b) for b in range(8)]
+        def product(dst, words, scales, t, rhs_words, rhs_scales):
+            nc.tensor.matmul_mx(
+                out=dst,
+                lhsT=words[:, t * P : (t + 1) * P].bitcast(FP8X4),
+                lhsT_scale=scales[:, t * P : (t + 1) * P],
+                rhs=rhs_words.bitcast(FP8X4),
+                rhs_scale=rhs_scales,
+                start=True,
+                stop=True,
+            )
+
+        banks = [psum.tile([P, 512], F32, name="bank%d" % b) for b in range(5)]
+        s_parts = [(0, halves[0], banks[0]), (0, halves[1], banks[1])] + [(t, slice(0, S), banks[t + 1]) for t in range(1, PACK)]
         s_window = [tile("s_window0", [P, S], F32)] + [tile("s_window%d" % t, [P, 2 * S], F32) for t in range(1, PACK)]
         s_plain = [s_window[t + 1][:, S:] for t in range(PACK - 1)] + [tile("s_plain3", [P, S], F32)[:]]
-        for u in range(2):
-            for t in range(PACK):
-                nc.tensor.matmul_mx(
-                    out=banks[2 * t + u][:, :half],
-                    lhsT=key_words[:, t * P : (t + 1) * P].bitcast(FP8X4),
-                    lhsT_scale=key_scales[:, t * P : (t + 1) * P],
-                    rhs=query_words[u][:].bitcast(FP8X4),
-                    rhs_scale=query_scales[:, u * half : (u + 1) * half],
-                    start=True,
-                    stop=True,
-                )
+        for t in range(PACK):
+            for u in range(2):
+                bank = banks[u] if t == 0 else banks[t + 1]
+                product(bank[:, halves[u]], key_words, key_scales, t, query_words[u][:], query_scales[:, halves[u]])
 
         a_window = [tile("a_window%d" % t, [P, S], F32) for t in range(PACK)]
         h_window = [tile("h_window%d" % t, [P, 2 * S], F32) for t in range(PACK)]
         w_grouped = tile("w_grouped", [P, N * PACK], BF16)
         w_words = tile("w_words", [P, N], U32)
         w_scales = tile("w_scales", [P, N], U8)
-        for t in range(PACK):
-            for u in range(2):
-                cols = slice(u * half, (u + 1) * half)
-                src = banks[2 * t + u][:, :half]
-                nc.scalar.activation(s_window[t][:, cols], src, ACT.Copy, scale=row_scale[:, t : t + 1])
-                nc.scalar.activation(s_plain[t][:, cols], src, ACT.Copy, scale=row_scale[:, t : t + 1])
-            if t == 0:
-                for u in range(2):
-                    cols = slice(u * half, (u + 1) * half)
-                    nc.vector.tensor_tensor(
-                        a_window[t][:, cols],
-                        s_window[t][:].indirect(entries(n1_sb, u * half, half)),
-                        s_plain[t][:, cols],
-                        ALU.subtract,
-                    )
+        for t, cols, bank in s_parts:
+            nc.scalar.activation(s_window[t][:, cols], bank[:, cols], ACT.Copy, scale=row_scale[:, t : t + 1])
+            if bank is banks[0]:
+                nc.vector.tensor_copy(s_plain[t][:, cols], s_window[t][:, cols])
             else:
-                nc.vector.tensor_tensor(a_window[t][:], s_window[t][:].indirect(n1_sb[:]), s_plain[t], ALU.subtract)
-            if t < 2:
-                m0, m1 = t * (P // 2), (t + 1) * (P // 2)
-                nc.vector.tensor_copy(
-                    w_grouped[:].rearrange("p (t m j) -> p m t j", t=PACK, j=PACK)[:, m0:m1],
-                    w_raw[:].rearrange("p j (m t) -> p m t j", t=PACK)[:, m0:m1],
+                nc.scalar.activation(s_plain[t][:, cols], bank[:, cols], ACT.Copy, scale=row_scale[:, t : t + 1])
+        for t, cols, bank in s_parts:
+            nc.vector.tensor_tensor(
+                a_window[t][:, cols],
+                s_window[t][:].indirect(entries(n1_sb, cols.start, cols.stop - cols.start)),
+                s_plain[t][:, cols],
+                ALU.subtract,
+            )
+        for first, count in PIECES:
+            for t in range(PACK):
+                nc.scalar.activation(
+                    h_window[t][:, S + first : S + first + count], a_window[t][:, first : first + count], ACT.Copy, scale=2.0
                 )
-            if t == 2:
-                nc.vector.quantize_mx(out=w_words[:].bitcast(FP8X4), scales=w_scales[:], in_=w_grouped[:])
-        for t in range(PACK):
-            nc.scalar.activation(h_window[t][:, S:], a_window[t][:], ACT.Copy, scale=2.0)
+        w_dst = w_grouped[:].rearrange("p (t m j) -> p m t j", t=PACK, j=PACK)
+        w_src = w_raw[:].rearrange("p j (m t) -> p m t j", t=PACK)
+        nc.vector.tensor_copy(w_dst[:, :W_SPLIT], w_src[:, :W_SPLIT])
+        nc.scalar.copy(w_dst[:, W_SPLIT:], w_src[:, W_SPLIT:])
+        nc.vector.quantize_mx(out=w_words[:].bitcast(FP8X4), scales=w_scales[:], in_=w_grouped[:])
 
-        h_banks = [psum.tile([P, 512], F32, name="bank%d" % b) for b in range(7)]
+        h_banks = [psum.tile([P, 512], F32, name="bank%d" % b) for b in (5, 6, 7, 0, 1, 2)]
         h_place = [
-            [h_banks[t // 2][:, (t % 2) * 256 : (t % 2 + 1) * 256] for t in range(PACK)],
-            [h_banks[2][:, t * 128 : (t + 1) * 128] for t in range(PACK)],
-            [h_banks[3 + t][:, :128] for t in range(PACK)],
+            [h_banks[t // 2][:, (t % 2) * half : (t % 2 + 1) * half] for t in range(PACK)],
+            [h_banks[2 + t][:, :half] for t in range(PACK)],
         ]
-        last = len(PIECES) - 1
-        for c, (first, count) in enumerate(PIECES):
-            cols = slice(first, first + count)
-            z_planes = tile("z_planes%d" % c, [P, PACK, count], F32)
+        st2_window = [tile("st2_window%d" % t, [P, 2 * S], F32) for t in range(PACK)]
+        shared = dict(tag="grouped_then_planes", align_bytes=64)
+        z_grouped = [sb.tile([P, half * PACK], BF16, name="z_grouped0", **shared), tile("z_grouped1", [P, half * PACK], BF16)]
+        z_words = [tile("z_words%d" % u, [P, half], U32) for u in range(2)]
+        z_scales = [tile("z_scales%d" % u, [P, half], U8) for u in range(2)]
+
+        def z_piece(c, z_planes, interleave):
+            first, count = PIECES[c]
             for t in range(PACK):
                 nc.vector.tensor_tensor(
-                    z_planes[:, t, :],
+                    z_planes[:, t * count : (t + 1) * count],
                     a_window[t][:].indirect(entries(n1_sb, first, count)),
                     h_window[t][:, S + first : S + first + count],
                     ALU.subtract,
                 )
-            z_grouped = tile("z_grouped%d" % c, [P, count * PACK], BF16)
-            dst = z_grouped[:].rearrange("p (c i t) -> p c t i", i=4, t=PACK)
-            src = z_planes[:].rearrange("p t (c i) -> p c t i", i=4)
-            if c == last:
-                nc.vector.tensor_copy(dst, src)
-            else:
-                nc.scalar.copy(dst, src)
-            z_words = tile("z_words%d" % c, [P, count], U32)
-            z_scales = tile("z_scales%d" % c, [P, count], U8)
-            nc.vector.quantize_mx(out=z_words[:].bitcast(FP8X4), scales=z_scales[:], in_=z_grouped[:])
+            at = (first % half) * PACK
+            interleave(
+                z_grouped[first // half][:, at : at + count * PACK].rearrange("p (c i t) -> p c t i", i=4, t=PACK),
+                z_planes[:].rearrange("p (t c i) -> p c t i", i=4, t=PACK),
+            )
+
+        def h_half(u):
+            nc.vector.quantize_mx(out=z_words[u][:].bitcast(FP8X4), scales=z_scales[u][:], in_=z_grouped[u][:])
             for t in range(PACK):
-                nc.tensor.matmul_mx(
-                    out=h_place[c][t],
-                    lhsT=w_words[:, t * P : (t + 1) * P].bitcast(FP8X4),
-                    lhsT_scale=w_scales[:, t * P : (t + 1) * P],
-                    rhs=z_words[:].bitcast(FP8X4),
-                    rhs_scale=z_scales[:],
-                    start=True,
-                    stop=True,
-                )
-            for t in range(PACK):
-                if c == last and t > 0:
-                    nc.vector.tensor_copy(h_window[t][:, cols], h_place[c][t])
-                else:
-                    nc.scalar.copy(h_window[t][:, cols], h_place[c][t])
+                product(h_place[u][t], w_words, w_scales, t, z_words[u][:], z_scales[u][:])
+            nc.scalar.activation(h_window[0][:, halves[u]], h_place[u][0], ACT.Sigmoid)
+            nc.scalar.copy(st2_window[0][:, S + u * half : S + (u + 1) * half], h_place[u][0])
+
+        z_piece(0, tile("z_planes0", [P, PACK * PIECES[0][1]], F32), nc.scalar.copy)
+        z_piece(1, tile("z_planes1", [P, PACK * PIECES[1][1]], F32), nc.scalar.copy)
+        h_half(0)
+        for t in range(1, PACK):
+            nc.scalar.copy(h_window[t][:, halves[0]], h_place[0][t])
+        z_piece(2, sb.tile([P, PACK * PIECES[2][1]], F32, name="z_planes2", **shared), nc.vector.tensor_copy)
+        h_half(1)
 
         out_rows = out.rearrange("(p t) j -> t p j", t=PACK)
-        for t in range(PACK):
-            st2_window = tile("st2_window%d" % t, [P, 2 * S], F32)
-            nc.scalar.activation(st2_window[:, S:], h_window[t][:].indirect(n2_sb[:]), ACT.Sigmoid)
-            nc.vector.tensor_tensor(st2_window[:, :S], h_window[t][:, :S], st2_window[:, S:], ALU.mult)
-            fetched = tile("fetched%d" % t, [P, S], F32)
-            nc.vector.tensor_copy(fetched[:], st2_window[:].indirect(n2_sb[:]))
-            result = tile("result%d" % t, [P, S], F32)
-            nc.vector.tensor_tensor(result[:], st2_window[:, :S], fetched[:], ALU.max)
-            nc.sync.dma_start(out_rows[t], result[:])
+        fetched = [tile("fetched%d" % t, [P, S], F32) for t in range(PACK)]
+        result = [h_window[t + 1][:, S:] for t in range(PACK - 1)] + [tile("result3", [P, S], F32)[:]]
+
+        def gate(t):
+            nc.scalar.copy(h_window[t][:, halves[1]], h_place[1][t])
+            nc.scalar.activation(st2_window[t][:, S:], h_window[t][:].indirect(n2_sb[:]), ACT.Sigmoid)
+            nc.vector.tensor_tensor(st2_window[t][:, :S], h_window[t][:, :S], st2_window[t][:, S:], ALU.mult)
+
+        def fetch(t, cols):
+            nc.vector.tensor_copy(
+                fetched[t][:, cols], st2_window[t][:].indirect(entries(n2_sb, cols.start, cols.stop - cols.start))
+            )
+
+        def finish(t, cols, queue):
+            nc.vector.tensor_tensor(result[t][:, cols], st2_window[t][:, cols], fetched[t][:, cols], ALU.max)
+            queue.dma_start(out_rows[t][:, cols], result[t][:, cols])
+
+        for u in range(2):
+            nc.vector.tensor_tensor(
+                st2_window[0][:, halves[u]],
+                h_window[0][:].indirect(entries(n2_sb, u * half, half)),
+                st2_window[0][:, S + u * half : S + (u + 1) * half],
+                ALU.mult,
+            )
+        for t in range(PACK - 1):
+            fetch(t, slice(0, S))
+            gate(t + 1)
+            finish(t, slice(0, S), nc.sync)
+        for u in range(2):
+            fetch(PACK - 1, halves[u])
+        finish(PACK - 1, halves[0], nc.sync)
+        finish(PACK - 1, halves[1], nc.scalar)

@@ -50,6 +50,7 @@ def tile_picked_keytwicetwicp_none_p_kernel(
         warm = tile("warm", [P, 8], F32)
         nc.vector.memset(d_scale_table[:].bitcast(I32), 0)
         nc.vector.memset(x_scale_table[:].bitcast(I32), 0)
+        nc.vector.memset(key_scales[:].bitcast(I32), 0)
         nc.gpsimd.memset(warm[:, 0:1], 0.0)
         nc.scalar.activation(warm[:, 4:5], warm[:, 0:1], ACT.Sigmoid)
 
@@ -59,29 +60,39 @@ def tile_picked_keytwicetwicp_none_p_kernel(
             nc.sync.dma_start(d_scale_table[a:P:16, :].bitcast(I32), d_rows[a])
         nc.sync.dma_start(offs_sb[:], offs)
         nc.sync.dma_start(d_table[:].bitcast(I32), d_words[0].rearrange("p n t -> p (n t)").bitcast(I32))
+        nc.sync.dma_start(x_table[:].bitcast(I32), x_words[0].rearrange("p n t -> p (n t)").bitcast(I32))
         x_rows = x_scales[0].bitcast(I32).rearrange("(q a) n -> a q n", a=4)
         for a in range(4):
             nc.scalar.dma_start(x_scale_table[a:P:32, :].bitcast(I32), x_rows[a])
-        nc.sync.dma_start(x_table[:].bitcast(I32), x_words[0].rearrange("p n t -> p (n t)").bitcast(I32))
-        nc.sync.dma_start(gain[:], gn.rearrange("(p t) o -> p (t o)", t=PACK))
         nc.sync.dma_start(n1_sb[:], n1)
         nc.sync.dma_start(n2_sb[:], n2)
+        nc.sync.dma_start(gain[:], gn.rearrange("(p t) o -> p (t o)", t=PACK))
 
-        d_scale_picked = tile("d_scale_picked", [P, H], U8)
-        nc.vector.tensor_copy(d_scale_picked[:], d_scale_table[:].indirect(kidx_sb[:]))
+        half = S // 2
+        halves = [slice(0, half), slice(half, S)]
+        d_scale_picked = [
+            tile("d_scale_picked0", [P, half], U8),
+            sb.tile([P, half], U8, name="d_scale_picked1", tag="picked_then_w", align_bytes=64),
+        ]
         d_scale_dealt = tile("d_scale_dealt", [P, H], U8)
-        nc.vector.tensor_copy(
-            d_scale_dealt[:].rearrange("p (t m) -> p m t", t=PACK),
-            d_scale_picked[:].rearrange("p (m t) -> p m t", t=PACK),
-        )
-        nc.vector.tensor_copy(key_scales[:].bitcast(I32), d_scale_dealt[:].bitcast(I32))
-        for a in range(2):
-            nc.scalar.dma_start(key_scales[2 + a : P : 32, :].bitcast(I32), d_scale_dealt[16 + a : P : 32, :].bitcast(I32))
+        for u in range(2):
+            nc.vector.tensor_copy(d_scale_picked[u][:], d_scale_table[:].indirect(entries(kidx_sb, u * half, half)))
+        for u in range(2):
+            nc.vector.tensor_copy(
+                d_scale_dealt[:].rearrange("p (t m) -> p m t", t=PACK)[:, u * half // PACK : (u + 1) * half // PACK],
+                d_scale_picked[u][:].rearrange("p (m t) -> p m t", t=PACK),
+            )
+        for a in range(4):
+            source = 16 * (a // 2) + a % 2
+            nc.scalar.dma_start(key_scales[a:P:32, :].bitcast(I32), d_scale_dealt[source:P:32, :].bitcast(I32))
 
+        w_rows = w1.rearrange("(p j) m -> p j m", j=PACK)
+        w_low = sb.tile([P, PACK, half], F32, name="w_low", tag="picked_then_w", align_bytes=64)
+        nc.sync.dma_start(w_low[:], w_rows[:, :, halves[0]])
         d_picked = tile("d_picked", [P, H], U32)
         nc.vector.tensor_copy(d_picked[:], d_table[:].indirect(kidx_sb[:]))
-        w_raw = sb.tile([P, PACK, N], F32, name="w_raw", tag="d_then_w", align_bytes=64)
-        nc.sync.dma_start(w_raw[:], w1.rearrange("(p j) m -> p j m", j=PACK))
+        w_high = sb.tile([P, PACK, half], F32, name="w_high", tag="d_then_w", align_bytes=64)
+        nc.sync.dma_start(w_high[:], w_rows[:, :, halves[1]])
         query_scales = tile("query_scales", [P, S], U8)
         nc.vector.tensor_copy(query_scales[:], x_scale_table[:].indirect(offs_sb[:]))
         key_words = tile("key_words", [P, H], U32)
@@ -89,8 +100,6 @@ def tile_picked_keytwicetwicp_none_p_kernel(
             key_words[:].rearrange("p (t m) -> p m t", t=PACK),
             d_picked[:].rearrange("p (m t) -> p m t", t=PACK),
         )
-        half = S // 2
-        halves = [slice(0, half), slice(half, S)]
         query_words = [
             sb.tile([P, half], U32, name="query_words0", tag="x_scales_then_words", align_bytes=64),
             tile("query_words1", [P, half], U32),
@@ -121,7 +130,7 @@ def tile_picked_keytwicetwicp_none_p_kernel(
                 bank = banks[u] if t == 0 else banks[t + 1]
                 product(bank[:, halves[u]], key_words, key_scales, t, query_words[u][:], query_scales[:, halves[u]])
 
-        a_window = [tile("a_window%d" % t, [P, S], F32) for t in range(PACK)]
+        a_window = [sb.tile([P, S], F32, name="a_window%d" % t, tag="a%d" % t, align_bytes=64) for t in range(PACK)]
         h_window = [tile("h_window%d" % t, [P, 2 * S], F32) for t in range(PACK)]
         w_grouped = tile("w_grouped", [P, N * PACK], BF16)
         w_words = tile("w_words", [P, N], U32)
@@ -145,23 +154,19 @@ def tile_picked_keytwicetwicp_none_p_kernel(
                     h_window[t][:, S + first : S + first + count], a_window[t][:, first : first + count], ACT.Copy, scale=2.0
                 )
         w_dst = w_grouped[:].rearrange("p (t m j) -> p m t j", t=PACK, j=PACK)
-        w_src = w_raw[:].rearrange("p j (m t) -> p m t j", t=PACK)
-        nc.vector.tensor_copy(w_dst[:, :W_SPLIT], w_src[:, :W_SPLIT])
-        nc.scalar.copy(w_dst[:, W_SPLIT:], w_src[:, W_SPLIT:])
+        nc.vector.tensor_copy(w_dst[:, :W_SPLIT], w_low[:].rearrange("p j (m t) -> p m t j", t=PACK))
+        nc.scalar.copy(w_dst[:, W_SPLIT:], w_high[:].rearrange("p j (m t) -> p m t j", t=PACK))
         nc.vector.quantize_mx(out=w_words[:].bitcast(FP8X4), scales=w_scales[:], in_=w_grouped[:])
 
-        h_banks = [psum.tile([P, 512], F32, name="bank%d" % b) for b in (5, 6, 7, 0, 1, 2)]
-        h_place = [
-            [h_banks[t // 2][:, (t % 2) * half : (t % 2 + 1) * half] for t in range(PACK)],
-            [h_banks[2 + t][:, :half] for t in range(PACK)],
-        ]
+        h_banks = [psum.tile([P, 512], F32, name="bank%d" % b) for b in (5, 6, 7, 0, 1, 2, 3)]
+        h_low = [h_banks[t // 2][:, (t % 2) * half : (t % 2 + 1) * half] for t in range(PACK)]
+        h_high = [None] + [h_banks[3 + t][:, :half] for t in range(1, PACK)]
         st2_window = [tile("st2_window%d" % t, [P, 2 * S], F32) for t in range(PACK)]
         shared = dict(tag="grouped_then_planes", align_bytes=64)
         z_grouped = [sb.tile([P, half * PACK], BF16, name="z_grouped0", **shared), tile("z_grouped1", [P, half * PACK], BF16)]
-        z_words = [tile("z_words%d" % u, [P, half], U32) for u in range(2)]
         z_scales = [tile("z_scales%d" % u, [P, half], U8) for u in range(2)]
 
-        def z_piece(c, z_planes, interleave):
+        def fetch_z(c, z_planes):
             first, count = PIECES[c]
             for t in range(PACK):
                 nc.vector.tensor_tensor(
@@ -170,33 +175,60 @@ def tile_picked_keytwicetwicp_none_p_kernel(
                     h_window[t][:, S + first : S + first + count],
                     ALU.subtract,
                 )
+
+        def group_z(c, z_planes, interleave):
+            first, count = PIECES[c]
             at = (first % half) * PACK
             interleave(
                 z_grouped[first // half][:, at : at + count * PACK].rearrange("p (c i t) -> p c t i", i=4, t=PACK),
                 z_planes[:].rearrange("p (t c i) -> p c t i", i=4, t=PACK),
             )
 
-        def h_half(u):
-            nc.vector.quantize_mx(out=z_words[u][:].bitcast(FP8X4), scales=z_scales[u][:], in_=z_grouped[u][:])
-            for t in range(PACK):
-                product(h_place[u][t], w_words, w_scales, t, z_words[u][:], z_scales[u][:])
-            nc.scalar.activation(h_window[0][:, halves[u]], h_place[u][0], ACT.Sigmoid)
-            nc.scalar.copy(st2_window[0][:, S + u * half : S + (u + 1) * half], h_place[u][0])
+        def quantize_z(c, words):
+            first, count = PIECES[c]
+            at = first % half
+            nc.vector.quantize_mx(
+                out=words[:, at : at + count].bitcast(FP8X4),
+                scales=z_scales[first // half][:, at : at + count],
+                in_=z_grouped[first // half][:, at * PACK : (at + count) * PACK],
+            )
 
-        z_piece(0, tile("z_planes0", [P, PACK * PIECES[0][1]], F32), nc.scalar.copy)
-        z_piece(1, tile("z_planes1", [P, PACK * PIECES[1][1]], F32), nc.scalar.copy)
-        h_half(0)
+        def first_tile(c, words, place):
+            first, count = PIECES[c]
+            at = first % half
+            product(place, w_words, w_scales, 0, words[:, at : at + count], z_scales[first // half][:, at : at + count])
+            nc.scalar.activation(h_window[0][:, first : first + count], place, ACT.Sigmoid)
+            nc.scalar.copy(st2_window[0][:, S + first : S + first + count], place)
+
+        z_planes = [tile("z_planes%d" % c, [P, PACK * PIECES[c][1]], F32) for c in range(2)]
+        for c in range(2):
+            fetch_z(c, z_planes[c])
+            group_z(c, z_planes[c], nc.scalar.copy)
+        z_words_low = tile("z_words_low", [P, half], U32)
+        quantize_z(0, z_words_low)
+        for t in range(PACK):
+            product(h_low[t], w_words, w_scales, t, z_words_low[:], z_scales[0][:])
+        nc.scalar.activation(h_window[0][:, halves[0]], h_low[0], ACT.Sigmoid)
+        nc.scalar.copy(st2_window[0][:, S : S + half], h_low[0])
         for t in range(1, PACK):
-            nc.scalar.copy(h_window[t][:, halves[0]], h_place[0][t])
-        z_piece(2, sb.tile([P, PACK * PIECES[2][1]], F32, name="z_planes2", **shared), nc.vector.tensor_copy)
-        h_half(1)
+            nc.scalar.copy(h_window[t][:, halves[0]], h_low[t])
+        last_planes = sb.tile([P, PACK * PIECES[2][1]], F32, name="z_planes2", **shared)
+        fetch_z(2, last_planes)
+        z_words_high = sb.tile([P, half], U32, name="z_words_high", tag="a2", align_bytes=64)
+        quantize_z(1, z_words_high)
+        group_z(2, last_planes, nc.vector.tensor_copy)
+        first_tile(1, z_words_high, h_banks[2][:, :128])
+        quantize_z(2, z_words_high)
+        first_tile(2, z_words_high, h_banks[3][:, :128])
+        for t in range(1, PACK):
+            product(h_high[t], w_words, w_scales, t, z_words_high[:], z_scales[1][:])
 
         out_rows = out.rearrange("(p t) j -> t p j", t=PACK)
         fetched = [tile("fetched%d" % t, [P, S], F32) for t in range(PACK)]
         result = [h_window[t + 1][:, S:] for t in range(PACK - 1)] + [tile("result3", [P, S], F32)[:]]
 
         def gate(t):
-            nc.scalar.copy(h_window[t][:, halves[1]], h_place[1][t])
+            nc.scalar.copy(h_window[t][:, halves[1]], h_high[t])
             nc.scalar.activation(st2_window[t][:, S:], h_window[t][:].indirect(n2_sb[:]), ACT.Sigmoid)
             nc.vector.tensor_tensor(st2_window[t][:, :S], h_window[t][:, :S], st2_window[t][:, S:], ALU.mult)
 

@@ -17,8 +17,16 @@ ACT = mybir.ActivationFunctionType
 
 P = 128
 PACK = 4
-W_SPLIT = 64
+QUADRANT = 32
+BLOCK_PARTITIONS = 8
+LIST_ROWS = 16
+LINE = 4
+BANK = 512
+HALF = S // 2
+HALVES = (slice(0, HALF), slice(HALF, S))
+WHOLE = slice(0, S)
 PIECES = ((0, 256), (256, 128), (384, 128))
+LAST = PACK - 1
 
 
 def tile_picked_keytwicetwicp_none_p_kernel(
@@ -33,82 +41,14 @@ def tile_picked_keytwicetwicp_none_p_kernel(
         def tile(name, shape, dtype):
             return sb.tile(shape, dtype, name=name, align_bytes=64)
 
-        def entries(list_tile, first, count):
-            return list_tile[:, first // 16 : (first + count) // 16]
+        def shared_tile(name, shape, dtype, tag):
+            return sb.tile(shape, dtype, name=name, tag=tag, align_bytes=64)
 
-        kidx_sb = lists.tile([P, H // 16], U16, name="kidx_sb")
-        offs_sb = lists.tile([P, S // 16], U16, name="offs_sb")
-        n1_sb = lists.tile([P, S // 16], U16, name="n1_sb")
-        n2_sb = lists.tile([P, S // 16], U16, name="n2_sb")
+        def entries(list_tile, cols):
+            return list_tile[:, cols.start // LIST_ROWS : cols.stop // LIST_ROWS]
 
-        d_scale_table = tile("d_scale_table", [P, G], U8)
-        x_scale_table = sb.tile([P, T], U8, name="x_scale_table", tag="x_scales_then_words", align_bytes=64)
-        key_scales = tile("key_scales", [P, H], U8)
-        d_table = sb.tile([P, G], U32, name="d_table", tag="d_then_w", align_bytes=64)
-        x_table = tile("x_table", [P, T], U32)
-        gain = tile("gain", [P, PACK], F32)
-        warm = tile("warm", [P, 8], F32)
-        nc.vector.memset(d_scale_table[:].bitcast(I32), 0)
-        nc.vector.memset(x_scale_table[:].bitcast(I32), 0)
-        nc.vector.memset(key_scales[:].bitcast(I32), 0)
-        nc.gpsimd.memset(warm[:, 0:1], 0.0)
-        nc.scalar.activation(warm[:, 4:5], warm[:, 0:1], ACT.Sigmoid)
-
-        nc.sync.dma_start(kidx_sb[:], kidx)
-        d_rows = d_scales[0].bitcast(I32).rearrange("(r a) n -> a r n", a=2)
-        for a in range(2):
-            nc.sync.dma_start(d_scale_table[a:P:16, :].bitcast(I32), d_rows[a])
-        nc.sync.dma_start(offs_sb[:], offs)
-        nc.sync.dma_start(d_table[:].bitcast(I32), d_words[0].rearrange("p n t -> p (n t)").bitcast(I32))
-        nc.sync.dma_start(x_table[:].bitcast(I32), x_words[0].rearrange("p n t -> p (n t)").bitcast(I32))
-        x_rows = x_scales[0].bitcast(I32).rearrange("(q a) n -> a q n", a=4)
-        for a in range(4):
-            nc.scalar.dma_start(x_scale_table[a:P:32, :].bitcast(I32), x_rows[a])
-        nc.sync.dma_start(n1_sb[:], n1)
-        nc.sync.dma_start(n2_sb[:], n2)
-        nc.sync.dma_start(gain[:], gn.rearrange("(p t) o -> p (t o)", t=PACK))
-
-        half = S // 2
-        halves = [slice(0, half), slice(half, S)]
-        d_scale_picked = [
-            tile("d_scale_picked0", [P, half], U8),
-            sb.tile([P, half], U8, name="d_scale_picked1", tag="picked_then_w", align_bytes=64),
-        ]
-        d_scale_dealt = tile("d_scale_dealt", [P, H], U8)
-        for u in range(2):
-            nc.vector.tensor_copy(d_scale_picked[u][:], d_scale_table[:].indirect(entries(kidx_sb, u * half, half)))
-        for u in range(2):
-            nc.vector.tensor_copy(
-                d_scale_dealt[:].rearrange("p (t m) -> p m t", t=PACK)[:, u * half // PACK : (u + 1) * half // PACK],
-                d_scale_picked[u][:].rearrange("p (m t) -> p m t", t=PACK),
-            )
-        for a in range(4):
-            source = 16 * (a // 2) + a % 2
-            nc.scalar.dma_start(key_scales[a:P:32, :].bitcast(I32), d_scale_dealt[source:P:32, :].bitcast(I32))
-
-        w_rows = w1.rearrange("(p j) m -> p j m", j=PACK)
-        w_low = sb.tile([P, PACK, half], F32, name="w_low", tag="picked_then_w", align_bytes=64)
-        nc.sync.dma_start(w_low[:], w_rows[:, :, halves[0]])
-        d_picked = tile("d_picked", [P, H], U32)
-        nc.vector.tensor_copy(d_picked[:], d_table[:].indirect(kidx_sb[:]))
-        w_high = sb.tile([P, PACK, half], F32, name="w_high", tag="d_then_w", align_bytes=64)
-        nc.sync.dma_start(w_high[:], w_rows[:, :, halves[1]])
-        query_scales = tile("query_scales", [P, S], U8)
-        nc.vector.tensor_copy(query_scales[:], x_scale_table[:].indirect(offs_sb[:]))
-        key_words = tile("key_words", [P, H], U32)
-        nc.vector.tensor_copy(
-            key_words[:].rearrange("p (t m) -> p m t", t=PACK),
-            d_picked[:].rearrange("p (m t) -> p m t", t=PACK),
-        )
-        query_words = [
-            sb.tile([P, half], U32, name="query_words0", tag="x_scales_then_words", align_bytes=64),
-            tile("query_words1", [P, half], U32),
-        ]
-        for u in range(2):
-            nc.vector.tensor_copy(query_words[u][:], x_table[:].indirect(entries(offs_sb, u * half, half)))
-
-        row_scale = tile("row_scale", [P, PACK], F32)
-        nc.scalar.activation(row_scale[:], gain[:], ACT.Copy, scale=1.0 / 32.0)
+        def upper(cols):
+            return slice(S + cols.start, S + cols.stop)
 
         def product(dst, words, scales, t, rhs_words, rhs_scales):
             nc.tensor.matmul_mx(
@@ -121,138 +61,209 @@ def tile_picked_keytwicetwicp_none_p_kernel(
                 stop=True,
             )
 
-        banks = [psum.tile([P, 512], F32, name="bank%d" % b) for b in range(5)]
-        s_parts = [(0, halves[0], banks[0]), (0, halves[1], banks[1])] + [(t, slice(0, S), banks[t + 1]) for t in range(1, PACK)]
-        s_window = [tile("s_window0", [P, S], F32)] + [tile("s_window%d" % t, [P, 2 * S], F32) for t in range(1, PACK)]
-        s_plain = [s_window[t + 1][:, S:] for t in range(PACK - 1)] + [tile("s_plain3", [P, S], F32)[:]]
+        kidx_sb = lists.tile([P, H // LIST_ROWS], U16, name="kidx_sb")
+        offs_sb = lists.tile([P, S // LIST_ROWS], U16, name="offs_sb")
+        n1_sb = lists.tile([P, S // LIST_ROWS], U16, name="n1_sb")
+        n2_sb = lists.tile([P, S // LIST_ROWS], U16, name="n2_sb")
+
+        d_scale_table = tile("d_scale_table", [P, G], U8)
+        x_scale_table = shared_tile("x_scale_table", [P, T], U8, "x_scales_then_words")
+        key_scales = tile("key_scales", [P, H], U8)
+        d_table = shared_tile("d_table", [P, G], U32, "d_then_w")
+        x_table = tile("x_table", [P, T], U32)
+        gain = tile("gain", [P, PACK], F32)
+        warm = tile("warm", [P, 8], F32)
+        nc.vector.memset(x_scale_table[:].bitcast(I32), 0)
+        nc.vector.memset(d_scale_table[:].bitcast(I32), 0)
+        nc.vector.memset(key_scales[:].bitcast(I32), 0)
+        nc.gpsimd.memset(warm[:, 0:1], 0.0)
+        nc.scalar.activation(warm[:, 4:5], warm[:, 0:1], ACT.Sigmoid)
+
+        nc.sync.dma_start(offs_sb[:], offs)
+        x_rows = x_scales[0].bitcast(I32).rearrange("(q a) n -> a q n", a=PACK)
+        for a in range(PACK):
+            nc.sync.dma_start(x_scale_table[a:P:QUADRANT, :].bitcast(I32), x_rows[a])
+        nc.sync.dma_start(d_scale_table[0:P:BLOCK_PARTITIONS, :].bitcast(I32), d_scales[0].bitcast(I32))
+        nc.sync.dma_start(kidx_sb[:], kidx)
+        nc.sync.dma_start(d_table[:].bitcast(I32), d_words[0].rearrange("p n t -> p (n t)").bitcast(I32))
+        nc.sync.dma_start(x_table[:].bitcast(I32), x_words[0].rearrange("p n t -> p (n t)").bitcast(I32))
+        nc.sync.dma_start(n1_sb[:], n1)
+        nc.sync.dma_start(n2_sb[:], n2)
+        nc.sync.dma_start(gain[:], gn.rearrange("(p t) o -> p (t o)", t=PACK))
+
+        d_scale_picked = [
+            tile("d_scale_picked0", [P, HALF], U8),
+            shared_tile("d_scale_picked1", [P, HALF], U8, "picked_then_w"),
+        ]
+        d_scale_dealt = tile("d_scale_dealt", [P, H], U8)
+        for u in range(2):
+            nc.vector.tensor_copy(d_scale_picked[u][:], d_scale_table[:].indirect(entries(kidx_sb, HALVES[u])))
+        for u in range(2):
+            nc.vector.tensor_copy(
+                d_scale_dealt[:].rearrange("p (t m) -> p m t", t=PACK)[:, u * HALF // PACK : (u + 1) * HALF // PACK],
+                d_scale_picked[u][:].rearrange("p (m t) -> p m t", t=PACK),
+            )
+        for a in range(PACK):
+            source = d_scale_dealt[BLOCK_PARTITIONS * a : P : QUADRANT, :]
+            nc.sync.dma_start(key_scales[a:P:QUADRANT, :].bitcast(I32), source.bitcast(I32))
+
+        w_rows = w1.rearrange("(p j) m -> p j m", j=PACK)
+        w_low = shared_tile("w_low", [P, PACK, HALF], F32, "picked_then_w")
+        nc.sync.dma_start(w_low[:], w_rows[:, :, HALVES[0]])
+        d_picked = tile("d_picked", [P, H], U32)
+        nc.vector.tensor_copy(d_picked[:], d_table[:].indirect(kidx_sb[:]))
+        w_high = shared_tile("w_high", [P, PACK, HALF], F32, "d_then_w")
+        nc.sync.dma_start(w_high[:], w_rows[:, :, HALVES[1]])
+        query_scales = tile("query_scales", [P, S], U8)
+        nc.vector.tensor_copy(query_scales[:], x_scale_table[:].indirect(offs_sb[:]))
+        key_words = tile("key_words", [P, H], U32)
+        nc.vector.tensor_copy(
+            key_words[:].rearrange("p (t m) -> p m t", t=PACK),
+            d_picked[:].rearrange("p (m t) -> p m t", t=PACK),
+        )
+        query_words = [
+            shared_tile("query_words0", [P, HALF], U32, "x_scales_then_words"),
+            tile("query_words1", [P, HALF], U32),
+        ]
+        for u in range(2):
+            nc.vector.tensor_copy(query_words[u][:], x_table[:].indirect(entries(offs_sb, HALVES[u])))
+
+        row_scale = tile("row_scale", [P, PACK], F32)
+        nc.scalar.activation(row_scale[:], gain[:], ACT.Copy, scale=1.0 / 32.0)
+
+        s_banks = [psum.tile([P, BANK], F32, name="bank%d" % b) for b in range(PACK + 1)]
+        s_parts = [(0, HALVES[u], s_banks[u]) for u in range(2)] + [(t, WHOLE, s_banks[t + 1]) for t in range(1, PACK)]
+        r_window = [tile("s_window0", [P, S], F32)] + [tile("s_window%d" % t, [P, 2 * S], F32) for t in range(1, PACK)]
+        r_plain = [r_window[t + 1][:, S:] for t in range(LAST)] + [tile("s_plain3", [P, S], F32)[:]]
         for t in range(PACK):
             for u in range(2):
-                bank = banks[u] if t == 0 else banks[t + 1]
-                product(bank[:, halves[u]], key_words, key_scales, t, query_words[u][:], query_scales[:, halves[u]])
+                bank = s_banks[u] if t == 0 else s_banks[t + 1]
+                product(bank[:, HALVES[u]], key_words, key_scales, t, query_words[u][:], query_scales[:, HALVES[u]])
 
-        a_window = [sb.tile([P, S], F32, name="a_window%d" % t, tag="a%d" % t, align_bytes=64) for t in range(PACK)]
+        a_window = [shared_tile("a_window%d" % t, [P, S], F32, "a%d" % t) for t in range(PACK)]
         h_window = [tile("h_window%d" % t, [P, 2 * S], F32) for t in range(PACK)]
         w_grouped = tile("w_grouped", [P, N * PACK], BF16)
         w_words = tile("w_words", [P, N], U32)
         w_scales = tile("w_scales", [P, N], U8)
-        for t, cols, bank in s_parts:
-            nc.scalar.activation(s_window[t][:, cols], bank[:, cols], ACT.Copy, scale=row_scale[:, t : t + 1])
-            if bank is banks[0]:
-                nc.vector.tensor_copy(s_plain[t][:, cols], s_window[t][:, cols])
+        for part, (t, cols, bank) in enumerate(s_parts):
+            nc.scalar.activation(r_window[t][:, cols], bank[:, cols], ACT.Copy, scale=row_scale[:, t : t + 1])
+            if part == 0:
+                nc.vector.tensor_copy(r_plain[t][:, cols], r_window[t][:, cols])
             else:
-                nc.scalar.activation(s_plain[t][:, cols], bank[:, cols], ACT.Copy, scale=row_scale[:, t : t + 1])
+                nc.scalar.activation(r_plain[t][:, cols], bank[:, cols], ACT.Copy, scale=row_scale[:, t : t + 1])
         for t, cols, bank in s_parts:
             nc.vector.tensor_tensor(
-                a_window[t][:, cols],
-                s_window[t][:].indirect(entries(n1_sb, cols.start, cols.stop - cols.start)),
-                s_plain[t][:, cols],
-                ALU.subtract,
+                a_window[t][:, cols], r_window[t][:].indirect(entries(n1_sb, cols)), r_plain[t][:, cols], ALU.subtract
             )
-        for first, count in PIECES:
+        piece_cols = [slice(first, first + count) for first, count in PIECES]
+        for cols in piece_cols:
             for t in range(PACK):
-                nc.scalar.activation(
-                    h_window[t][:, S + first : S + first + count], a_window[t][:, first : first + count], ACT.Copy, scale=2.0
-                )
-        w_dst = w_grouped[:].rearrange("p (t m j) -> p m t j", t=PACK, j=PACK)
-        nc.vector.tensor_copy(w_dst[:, :W_SPLIT], w_low[:].rearrange("p j (m t) -> p m t j", t=PACK))
-        nc.scalar.copy(w_dst[:, W_SPLIT:], w_high[:].rearrange("p j (m t) -> p m t j", t=PACK))
+                nc.scalar.activation(h_window[t][:, upper(cols)], a_window[t][:, cols], ACT.Copy, scale=2.0)
+
+        w_dealt = w_grouped[:].rearrange("p (t m j) -> p m t j", t=PACK, j=PACK)
+        nc.vector.tensor_copy(w_dealt[:, : HALF // PACK], w_low[:].rearrange("p j (m t) -> p m t j", t=PACK))
+        nc.scalar.copy(w_dealt[:, HALF // PACK :], w_high[:].rearrange("p j (m t) -> p m t j", t=PACK))
         nc.vector.quantize_mx(out=w_words[:].bitcast(FP8X4), scales=w_scales[:], in_=w_grouped[:])
 
-        h_banks = [psum.tile([P, 512], F32, name="bank%d" % b) for b in (5, 6, 7, 0, 1, 2, 3)]
-        h_low = [h_banks[t // 2][:, (t % 2) * half : (t % 2 + 1) * half] for t in range(PACK)]
-        h_high = [None] + [h_banks[3 + t][:, :half] for t in range(1, PACK)]
+        h_banks = [psum.tile([P, BANK], F32, name="bank%d" % b) for b in (5, 6, 7, 0, 1, 2, 3)]
+        h_low = [h_banks[t // 2][:, HALVES[t % 2]] for t in range(PACK)]
+        h_first_tile = {c: h_banks[1 + c][:, : PIECES[c][1]] for c in (1, 2)}
+        h_high = {t: h_banks[3 + t][:, :HALF] for t in range(1, PACK)}
         st2_window = [tile("st2_window%d" % t, [P, 2 * S], F32) for t in range(PACK)]
-        shared = dict(tag="grouped_then_planes", align_bytes=64)
-        z_grouped = [sb.tile([P, half * PACK], BF16, name="z_grouped0", **shared), tile("z_grouped1", [P, half * PACK], BF16)]
-        z_scales = [tile("z_scales%d" % u, [P, half], U8) for u in range(2)]
+        z_grouped = [
+            shared_tile("z_grouped0", [P, HALF * PACK], BF16, "grouped_then_planes"),
+            tile("z_grouped1", [P, HALF * PACK], BF16),
+        ]
+        z_scales = [tile("z_scales%d" % u, [P, HALF], U8) for u in range(2)]
 
-        def fetch_z(c, z_planes):
+        def in_half(c):
             first, count = PIECES[c]
+            return first // HALF, slice(first % HALF, first % HALF + count)
+
+        def fetch_z(c, planes):
+            count = PIECES[c][1]
             for t in range(PACK):
                 nc.vector.tensor_tensor(
-                    z_planes[:, t * count : (t + 1) * count],
-                    a_window[t][:].indirect(entries(n1_sb, first, count)),
-                    h_window[t][:, S + first : S + first + count],
+                    planes[:, t * count : (t + 1) * count],
+                    a_window[t][:].indirect(entries(n1_sb, piece_cols[c])),
+                    h_window[t][:, upper(piece_cols[c])],
                     ALU.subtract,
                 )
 
-        def group_z(c, z_planes, interleave):
-            first, count = PIECES[c]
-            at = (first % half) * PACK
-            interleave(
-                z_grouped[first // half][:, at : at + count * PACK].rearrange("p (c i t) -> p c t i", i=4, t=PACK),
-                z_planes[:].rearrange("p (t c i) -> p c t i", i=4, t=PACK),
+        def group_z(c, planes, copy):
+            u, within = in_half(c)
+            copy(
+                z_grouped[u][:, within.start * PACK : within.stop * PACK].rearrange("p (c i t) -> p c t i", i=LINE, t=PACK),
+                planes[:].rearrange("p (t c i) -> p c t i", i=LINE, t=PACK),
             )
 
         def quantize_z(c, words):
-            first, count = PIECES[c]
-            at = first % half
+            u, within = in_half(c)
             nc.vector.quantize_mx(
-                out=words[:, at : at + count].bitcast(FP8X4),
-                scales=z_scales[first // half][:, at : at + count],
-                in_=z_grouped[first // half][:, at * PACK : (at + count) * PACK],
+                out=words[:, within].bitcast(FP8X4),
+                scales=z_scales[u][:, within],
+                in_=z_grouped[u][:, within.start * PACK : within.stop * PACK],
             )
 
-        def first_tile(c, words, place):
-            first, count = PIECES[c]
-            at = first % half
-            product(place, w_words, w_scales, 0, words[:, at : at + count], z_scales[first // half][:, at : at + count])
-            nc.scalar.activation(h_window[0][:, first : first + count], place, ACT.Sigmoid)
-            nc.scalar.copy(st2_window[0][:, S + first : S + first + count], place)
+        def leave_first_tile(c, place):
+            nc.scalar.activation(h_window[0][:, piece_cols[c]], place, ACT.Sigmoid)
+            nc.scalar.copy(st2_window[0][:, upper(piece_cols[c])], place)
+
+        def first_tile_of_piece(c, words):
+            u, within = in_half(c)
+            product(h_first_tile[c], w_words, w_scales, 0, words[:, within], z_scales[u][:, within])
+            leave_first_tile(c, h_first_tile[c])
 
         z_planes = [tile("z_planes%d" % c, [P, PACK * PIECES[c][1]], F32) for c in range(2)]
         for c in range(2):
             fetch_z(c, z_planes[c])
             group_z(c, z_planes[c], nc.scalar.copy)
-        z_words_low = tile("z_words_low", [P, half], U32)
+        z_words_low = tile("z_words_low", [P, HALF], U32)
         quantize_z(0, z_words_low)
         for t in range(PACK):
             product(h_low[t], w_words, w_scales, t, z_words_low[:], z_scales[0][:])
-        nc.scalar.activation(h_window[0][:, halves[0]], h_low[0], ACT.Sigmoid)
-        nc.scalar.copy(st2_window[0][:, S : S + half], h_low[0])
+        leave_first_tile(0, h_low[0])
         for t in range(1, PACK):
-            nc.scalar.copy(h_window[t][:, halves[0]], h_low[t])
-        last_planes = sb.tile([P, PACK * PIECES[2][1]], F32, name="z_planes2", **shared)
+            nc.scalar.copy(h_window[t][:, HALVES[0]], h_low[t])
+        last_planes = shared_tile("z_planes2", [P, PACK * PIECES[2][1]], F32, "grouped_then_planes")
         fetch_z(2, last_planes)
-        z_words_high = sb.tile([P, half], U32, name="z_words_high", tag="a2", align_bytes=64)
+        z_words_high = shared_tile("z_words_high", [P, HALF], U32, "a2")
         quantize_z(1, z_words_high)
         group_z(2, last_planes, nc.vector.tensor_copy)
-        first_tile(1, z_words_high, h_banks[2][:, :128])
+        first_tile_of_piece(1, z_words_high)
         quantize_z(2, z_words_high)
-        first_tile(2, z_words_high, h_banks[3][:, :128])
+        first_tile_of_piece(2, z_words_high)
         for t in range(1, PACK):
             product(h_high[t], w_words, w_scales, t, z_words_high[:], z_scales[1][:])
 
         out_rows = out.rearrange("(p t) j -> t p j", t=PACK)
         fetched = [tile("fetched%d" % t, [P, S], F32) for t in range(PACK)]
-        result = [h_window[t + 1][:, S:] for t in range(PACK - 1)] + [tile("result3", [P, S], F32)[:]]
+        result = [h_window[t + 1][:, S:] for t in range(LAST)] + [tile("result3", [P, S], F32)[:]]
 
         def gate(t):
-            nc.scalar.copy(h_window[t][:, halves[1]], h_high[t])
+            nc.scalar.copy(h_window[t][:, HALVES[1]], h_high[t])
             nc.scalar.activation(st2_window[t][:, S:], h_window[t][:].indirect(n2_sb[:]), ACT.Sigmoid)
             nc.vector.tensor_tensor(st2_window[t][:, :S], h_window[t][:, :S], st2_window[t][:, S:], ALU.mult)
 
         def fetch(t, cols):
-            nc.vector.tensor_copy(
-                fetched[t][:, cols], st2_window[t][:].indirect(entries(n2_sb, cols.start, cols.stop - cols.start))
-            )
+            nc.vector.tensor_copy(fetched[t][:, cols], st2_window[t][:].indirect(entries(n2_sb, cols)))
 
         def finish(t, cols, queue):
             nc.vector.tensor_tensor(result[t][:, cols], st2_window[t][:, cols], fetched[t][:, cols], ALU.max)
             queue.dma_start(out_rows[t][:, cols], result[t][:, cols])
 
-        for u in range(2):
+        for cols in HALVES:
             nc.vector.tensor_tensor(
-                st2_window[0][:, halves[u]],
-                h_window[0][:].indirect(entries(n2_sb, u * half, half)),
-                st2_window[0][:, S + u * half : S + (u + 1) * half],
+                st2_window[0][:, cols],
+                h_window[0][:].indirect(entries(n2_sb, cols)),
+                st2_window[0][:, upper(cols)],
                 ALU.mult,
             )
-        for t in range(PACK - 1):
-            fetch(t, slice(0, S))
+        for t in range(LAST):
+            fetch(t, WHOLE)
             gate(t + 1)
-            finish(t, slice(0, S), nc.sync)
-        for u in range(2):
-            fetch(PACK - 1, halves[u])
-        finish(PACK - 1, halves[0], nc.sync)
-        finish(PACK - 1, halves[1], nc.scalar)
+            finish(t, WHOLE, nc.sync)
+        for cols in HALVES:
+            fetch(LAST, cols)
+        finish(LAST, HALVES[0], nc.sync)
+        finish(LAST, HALVES[1], nc.scalar)

from contextlib import ExitStack

import concourse.mybir as mybir

K, T, S, N, G, H = 512, 2048, 512, 512, 2048, 512
FLOPS = 2 * K * H * S + 2 * H * N * S

F32 = mybir.dt.float32
BF16 = mybir.dt.bfloat16
I32 = mybir.dt.int32
U32 = mybir.dt.uint32
U16 = mybir.dt.uint16
U8 = mybir.dt.uint8
FP8X4 = mybir.dt.float8_e4m3fn_x4
ALU = mybir.AluOpType
ACT = mybir.ActivationFunctionType

P = 128
PACK = 4
QUADRANT = 32
BLOCK_PARTITIONS = 8
LIST_ROWS = 16
LINE = 4
BANK = 512
HALF = S // 2
HALVES = (slice(0, HALF), slice(HALF, S))
WHOLE = slice(0, S)
PIECES = ((0, 256), (256, 128), (384, 128))
LAST = PACK - 1


def tile_picked_keytwicetwicp_none_p_kernel(
    tc, x_words, x_scales, d_words, d_scales, gn, w1, offs, kidx, n1, n2, out
):
    nc = tc.nc
    with ExitStack() as ctx:
        lists = ctx.enter_context(tc.tile_pool(name="lists", bufs=1))
        sb = ctx.enter_context(tc.tile_pool(name="sb", bufs=1))
        psum = ctx.enter_context(tc.psum_pool(name="psum", bufs=1))

        def tile(name, shape, dtype):
            return sb.tile(shape, dtype, name=name, align_bytes=64)

        def shared_tile(name, shape, dtype, tag):
            return sb.tile(shape, dtype, name=name, tag=tag, align_bytes=64)

        def entries(list_tile, cols):
            return list_tile[:, cols.start // LIST_ROWS : cols.stop // LIST_ROWS]

        def upper(cols):
            return slice(S + cols.start, S + cols.stop)

        def product(dst, words, scales, t, rhs_words, rhs_scales):
            nc.tensor.matmul_mx(
                out=dst,
                lhsT=words[:, t * P : (t + 1) * P].bitcast(FP8X4),
                lhsT_scale=scales[:, t * P : (t + 1) * P],
                rhs=rhs_words.bitcast(FP8X4),
                rhs_scale=rhs_scales,
                start=True,
                stop=True,
            )

        kidx_sb = lists.tile([P, H // LIST_ROWS], U16, name="kidx_sb")
        offs_sb = lists.tile([P, S // LIST_ROWS], U16, name="offs_sb")
        n1_sb = lists.tile([P, S // LIST_ROWS], U16, name="n1_sb")
        n2_sb = lists.tile([P, S // LIST_ROWS], U16, name="n2_sb")

        d_scale_table = tile("d_scale_table", [P, G], U8)
        x_scale_table = shared_tile("x_scale_table", [P, T], U8, "x_scales_then_words")
        key_scales = tile("key_scales", [P, H], U8)
        d_table = shared_tile("d_table", [P, G], U32, "d_then_w")
        x_table = tile("x_table", [P, T], U32)
        gain = tile("gain", [P, PACK], F32)
        warm = tile("warm", [P, 8], F32)
        nc.vector.memset(x_scale_table[:].bitcast(I32), 0)
        nc.vector.memset(d_scale_table[:].bitcast(I32), 0)
        nc.vector.memset(key_scales[:].bitcast(I32), 0)
        nc.gpsimd.memset(warm[:, 0:1], 0.0)
        nc.scalar.activation(warm[:, 4:5], warm[:, 0:1], ACT.Sigmoid)

        nc.sync.dma_start(offs_sb[:], offs)
        x_rows = x_scales[0].bitcast(I32).rearrange("(q a) n -> a q n", a=PACK)
        for a in range(PACK):
            nc.sync.dma_start(x_scale_table[a:P:QUADRANT, :].bitcast(I32), x_rows[a])
        nc.sync.dma_start(d_scale_table[0:P:BLOCK_PARTITIONS, :].bitcast(I32), d_scales[0].bitcast(I32))
        nc.sync.dma_start(kidx_sb[:], kidx)
        nc.sync.dma_start(d_table[:].bitcast(I32), d_words[0].rearrange("p n t -> p (n t)").bitcast(I32))
        nc.sync.dma_start(x_table[:].bitcast(I32), x_words[0].rearrange("p n t -> p (n t)").bitcast(I32))
        nc.sync.dma_start(n1_sb[:], n1)
        nc.sync.dma_start(n2_sb[:], n2)
        nc.sync.dma_start(gain[:], gn.rearrange("(p t) o -> p (t o)", t=PACK))

        d_scale_picked = [
            tile("d_scale_picked0", [P, HALF], U8),
            shared_tile("d_scale_picked1", [P, HALF], U8, "picked_then_w"),
        ]
        d_scale_dealt = tile("d_scale_dealt", [P, H], U8)
        for u in range(2):
            nc.vector.tensor_copy(d_scale_picked[u][:], d_scale_table[:].indirect(entries(kidx_sb, HALVES[u])))
        for u in range(2):
            nc.vector.tensor_copy(
                d_scale_dealt[:].rearrange("p (t m) -> p m t", t=PACK)[:, u * HALF // PACK : (u + 1) * HALF // PACK],
                d_scale_picked[u][:].rearrange("p (m t) -> p m t", t=PACK),
            )
        for a in range(PACK):
            source = d_scale_dealt[BLOCK_PARTITIONS * a : P : QUADRANT, :]
            nc.sync.dma_start(key_scales[a:P:QUADRANT, :].bitcast(I32), source.bitcast(I32))

        w_rows = w1.rearrange("(p j) m -> p j m", j=PACK)
        w_low = shared_tile("w_low", [P, PACK, HALF], F32, "picked_then_w")
        nc.sync.dma_start(w_low[:], w_rows[:, :, HALVES[0]])
        d_picked = tile("d_picked", [P, H], U32)
        nc.vector.tensor_copy(d_picked[:], d_table[:].indirect(kidx_sb[:]))
        w_high = shared_tile("w_high", [P, PACK, HALF], F32, "d_then_w")
        nc.sync.dma_start(w_high[:], w_rows[:, :, HALVES[1]])
        query_scales = tile("query_scales", [P, S], U8)
        nc.vector.tensor_copy(query_scales[:], x_scale_table[:].indirect(offs_sb[:]))
        key_words = tile("key_words", [P, H], U32)
        nc.vector.tensor_copy(
            key_words[:].rearrange("p (t m) -> p m t", t=PACK),
            d_picked[:].rearrange("p (m t) -> p m t", t=PACK),
        )
        query_words = [
            shared_tile("query_words0", [P, HALF], U32, "x_scales_then_words"),
            tile("query_words1", [P, HALF], U32),
        ]
        for u in range(2):
            nc.vector.tensor_copy(query_words[u][:], x_table[:].indirect(entries(offs_sb, HALVES[u])))

        row_scale = tile("row_scale", [P, PACK], F32)
        nc.scalar.activation(row_scale[:], gain[:], ACT.Copy, scale=1.0 / 32.0)

        s_banks = [psum.tile([P, BANK], F32, name="bank%d" % b) for b in range(PACK + 1)]
        s_parts = [(0, HALVES[u], s_banks[u]) for u in range(2)] + [(t, WHOLE, s_banks[t + 1]) for t in range(1, PACK)]
        r_window = [tile("s_window0", [P, S], F32)] + [tile("s_window%d" % t, [P, 2 * S], F32) for t in range(1, PACK)]
        r_plain = [r_window[t + 1][:, S:] for t in range(LAST)] + [tile("s_plain3", [P, S], F32)[:]]
        for t in range(PACK):
            for u in range(2):
                bank = s_banks[u] if t == 0 else s_banks[t + 1]
                product(bank[:, HALVES[u]], key_words, key_scales, t, query_words[u][:], query_scales[:, HALVES[u]])

        a_window = [shared_tile("a_window%d" % t, [P, S], F32, "a%d" % t) for t in range(PACK)]
        h_window = [tile("h_window%d" % t, [P, 2 * S], F32) for t in range(PACK)]
        w_grouped = tile("w_grouped", [P, N * PACK], BF16)
        w_words = tile("w_words", [P, N], U32)
        w_scales = tile("w_scales", [P, N], U8)
        for part, (t, cols, bank) in enumerate(s_parts):
            nc.scalar.activation(r_window[t][:, cols], bank[:, cols], ACT.Copy, scale=row_scale[:, t : t + 1])
            if part == 0:
                nc.vector.tensor_copy(r_plain[t][:, cols], r_window[t][:, cols])
            else:
                nc.scalar.activation(r_plain[t][:, cols], bank[:, cols], ACT.Copy, scale=row_scale[:, t : t + 1])
        for t, cols, bank in s_parts:
            nc.vector.tensor_tensor(
                a_window[t][:, cols], r_window[t][:].indirect(entries(n1_sb, cols)), r_plain[t][:, cols], ALU.subtract
            )
        piece_cols = [slice(first, first + count) for first, count in PIECES]
        for cols in piece_cols:
            for t in range(PACK):
                nc.scalar.activation(h_window[t][:, upper(cols)], a_window[t][:, cols], ACT.Copy, scale=2.0)

        w_dealt = w_grouped[:].rearrange("p (t m j) -> p m t j", t=PACK, j=PACK)
        nc.vector.tensor_copy(w_dealt[:, : HALF // PACK], w_low[:].rearrange("p j (m t) -> p m t j", t=PACK))
        nc.scalar.copy(w_dealt[:, HALF // PACK :], w_high[:].rearrange("p j (m t) -> p m t j", t=PACK))
        nc.vector.quantize_mx(out=w_words[:].bitcast(FP8X4), scales=w_scales[:], in_=w_grouped[:])

        h_banks = [psum.tile([P, BANK], F32, name="bank%d" % b) for b in (5, 6, 7, 0, 1, 2, 3)]
        h_low = [h_banks[t // 2][:, HALVES[t % 2]] for t in range(PACK)]
        h_first_tile = {c: h_banks[1 + c][:, : PIECES[c][1]] for c in (1, 2)}
        h_high = {t: h_banks[3 + t][:, :HALF] for t in range(1, PACK)}
        st2_window = [tile("st2_window%d" % t, [P, 2 * S], F32) for t in range(PACK)]
        z_grouped = [
            shared_tile("z_grouped0", [P, HALF * PACK], BF16, "grouped_then_planes"),
            tile("z_grouped1", [P, HALF * PACK], BF16),
        ]
        z_scales = [tile("z_scales%d" % u, [P, HALF], U8) for u in range(2)]

        def in_half(c):
            first, count = PIECES[c]
            return first // HALF, slice(first % HALF, first % HALF + count)

        def fetch_z(c, planes):
            count = PIECES[c][1]
            for t in range(PACK):
                nc.vector.tensor_tensor(
                    planes[:, t * count : (t + 1) * count],
                    a_window[t][:].indirect(entries(n1_sb, piece_cols[c])),
                    h_window[t][:, upper(piece_cols[c])],
                    ALU.subtract,
                )

        def group_z(c, planes, copy):
            u, within = in_half(c)
            copy(
                z_grouped[u][:, within.start * PACK : within.stop * PACK].rearrange("p (c i t) -> p c t i", i=LINE, t=PACK),
                planes[:].rearrange("p (t c i) -> p c t i", i=LINE, t=PACK),
            )

        def quantize_z(c, words):
            u, within = in_half(c)
            nc.vector.quantize_mx(
                out=words[:, within].bitcast(FP8X4),
                scales=z_scales[u][:, within],
                in_=z_grouped[u][:, within.start * PACK : within.stop * PACK],
            )

        def leave_first_tile(c, place):
            nc.scalar.activation(h_window[0][:, piece_cols[c]], place, ACT.Sigmoid)
            nc.scalar.copy(st2_window[0][:, upper(piece_cols[c])], place)

        def first_tile_of_piece(c, words):
            u, within = in_half(c)
            product(h_first_tile[c], w_words, w_scales, 0, words[:, within], z_scales[u][:, within])
            leave_first_tile(c, h_first_tile[c])

        z_planes = [tile("z_planes%d" % c, [P, PACK * PIECES[c][1]], F32) for c in range(2)]
        for c in range(2):
            fetch_z(c, z_planes[c])
            group_z(c, z_planes[c], nc.scalar.copy)
        z_words_low = tile("z_words_low", [P, HALF], U32)
        quantize_z(0, z_words_low)
        for t in range(PACK):
            product(h_low[t], w_words, w_scales, t, z_words_low[:], z_scales[0][:])
        leave_first_tile(0, h_low[0])
        for t in range(1, PACK):
            nc.scalar.copy(h_window[t][:, HALVES[0]], h_low[t])
        last_planes = shared_tile("z_planes2", [P, PACK * PIECES[2][1]], F32, "grouped_then_planes")
        fetch_z(2, last_planes)
        z_words_high = shared_tile("z_words_high", [P, HALF], U32, "a2")
        quantize_z(1, z_words_high)
        group_z(2, last_planes, nc.vector.tensor_copy)
        first_tile_of_piece(1, z_words_high)
        quantize_z(2, z_words_high)
        first_tile_of_piece(2, z_words_high)
        for t in range(1, PACK):
            product(h_high[t], w_words, w_scales, t, z_words_high[:], z_scales[1][:])

        out_rows = out.rearrange("(p t) j -> t p j", t=PACK)
        fetched = [tile("fetched%d" % t, [P, S], F32) for t in range(PACK)]
        result = [h_window[t + 1][:, S:] for t in range(LAST)] + [tile("result3", [P, S], F32)[:]]

        def gate(t):
            nc.scalar.copy(h_window[t][:, HALVES[1]], h_high[t])
            nc.scalar.activation(st2_window[t][:, S:], h_window[t][:].indirect(n2_sb[:]), ACT.Sigmoid)
            nc.vector.tensor_tensor(st2_window[t][:, :S], h_window[t][:, :S], st2_window[t][:, S:], ALU.mult)

        def fetch(t, cols):
            nc.vector.tensor_copy(fetched[t][:, cols], st2_window[t][:].indirect(entries(n2_sb, cols)))

        def finish(t, cols, queue):
            nc.vector.tensor_tensor(result[t][:, cols], st2_window[t][:, cols], fetched[t][:, cols], ALU.max)
            queue.dma_start(out_rows[t][:, cols], result[t][:, cols])

        for cols in HALVES:
            nc.vector.tensor_tensor(
                st2_window[0][:, cols],
                h_window[0][:].indirect(entries(n2_sb, cols)),
                st2_window[0][:, upper(cols)],
                ALU.mult,
            )
        for t in range(LAST):
            fetch(t, WHOLE)
            gate(t + 1)
            finish(t, WHOLE, nc.sync)
        for cols in HALVES:
            fetch(LAST, cols)
        finish(LAST, HALVES[0], nc.sync)
        finish(LAST, HALVES[1], nc.scalar)
